import numpy as np
import ml_dtypes


def mxq(x, axis, fmt="e4m3"):
    dtype, down = {"e4m3": (ml_dtypes.float8_e4m3fn, 7), "e5m2": (ml_dtypes.float8_e5m2, 14)}[fmt]
    v = np.moveaxis(np.asarray(x, np.float32).astype(ml_dtypes.bfloat16).astype(np.float64), axis, -1)
    blocks = v.reshape(v.shape[:-1] + (-1, 32))
    amax = np.abs(blocks).max(-1, keepdims=True)
    byte = np.maximum(np.where(amax > 0, np.frexp(amax)[1] - 1 + 127, 0) - down, 1)
    scale = np.exp2(byte - 127.0)
    codes = (blocks / scale).astype(np.float32).astype(dtype).astype(np.float64)
    return np.moveaxis((codes * scale).reshape(v.shape), -1, axis)


WIDE = False


def mx_kscale(k):
    if not WIDE:
        return np.ones(k)
    levels = np.array([10, -10, 5, -5, 0])
    if k % 512:
        return np.exp2(np.random.permutation(np.resize(levels, k // 32))).repeat(32)
    a = np.empty((k // 512, 16))
    for p in range(k // 512):
        a[p, :8] = np.random.permutation(np.resize(levels, 8))
        for g in range(8):
            far = levels[np.abs(levels - a[p, g]) >= 10]
            a[p, g + 8] = far[np.random.randint(len(far))]
    return np.exp2(a.ravel()).repeat(32)


def f64(x):
    return np.asarray(x).astype(np.float64)


def striped(idx):
    return np.tile(np.asarray(idx).reshape(-1, 16).T, (8, 1)).astype(np.uint16)


def unstriped(offs):
    return offs[:16].T.reshape(-1).astype(np.int64)


E2M1 = np.array([0.0, 0.5, 1.0, 1.5, 2.0, 3.0, 4.0, 6.0, -0.0, -0.5, -1.0, -1.5, -2.0, -3.0, -4.0, -6.0])


def pack_weight(w, fmt):
    k, n = w.shape
    w = f64(np.asarray(w, np.float32).astype(ml_dtypes.bfloat16)).reshape(k // 32, 32, n)
    amax = np.abs(w).max(1)
    if fmt == "e4m3":
        byte = np.frexp(amax)[1] - 1 + 127 - 7
    else:
        mant, ex = np.frexp(amax / 6.0)
        byte = np.where(mant > 0.5, ex, ex - 1) + 127
    byte = np.clip(np.where(amax > 0, byte, 1), 1, 254)
    scaled = (w * np.exp2(127.0 - byte)[:, None, :]).reshape(k, n).astype(np.float32)
    by_word = np.ascontiguousarray(scaled.reshape(k // 512, 128, 4, n).transpose(0, 1, 3, 2))
    if fmt == "e4m3":
        words = by_word.astype(ml_dtypes.float8_e4m3fn).view(np.uint8)
    else:
        c = by_word.astype(ml_dtypes.float4_e2m1fn).view(np.uint8) & 0xF
        words = (c[..., 0::2] | (c[..., 1::2] << 4)).reshape(k // 512, 128, 2 * n)
    return np.ascontiguousarray(words), np.ascontiguousarray(byte.astype(np.uint8).reshape(k // 512, 16, n))


def unpack_weight(words, scales, fmt):
    g, _, n = scales.shape
    words = np.ascontiguousarray(words).reshape(g, 128, n, -1)
    if fmt == "e4m3":
        vals = words.view(ml_dtypes.float8_e4m3fn).astype(np.float64)
    else:
        nib = np.empty((g, 128, n, 4), np.uint8)
        nib[..., 0::2] = words & 0xF
        nib[..., 1::2] = words >> 4
        vals = E2M1[nib]
    vals = vals * np.repeat(np.exp2(scales.astype(np.float64) - 127.0), 8, axis=1)[..., None]
    return vals.transpose(0, 1, 3, 2).reshape(g * 512, n)


def softplus(v):
    return np.log(1.0 + np.exp(v))


def bf(x):
    return np.asarray(x, np.float32).astype(ml_dtypes.bfloat16)


def planes(Y):
    r, m = Y.shape
    b = f64(bf(Y)).reshape(r // 32, 32, m)
    amax = np.abs(b).max(1)
    byte = np.clip(np.where(amax > 0, np.frexp(amax)[1] - 1 + 127 - 7, 1), 1, 254)
    codes = (b * np.exp2(127.0 - byte)[:, None, :]).reshape(r, m).astype(np.float32).astype(ml_dtypes.float8_e4m3fn).view(np.uint8)
    words = codes.reshape(r // 512, 128, 4, m).transpose(0, 1, 3, 2)
    return np.ascontiguousarray(words), np.ascontiguousarray(byte.astype(np.uint8).reshape(r // 512, 16, m))


K, T, J, N = 512, 2048, 512, 512


def setup_inputs():
    n = np.random.standard_normal
    idx = np.random.permutation(T)[:J]
    idx2 = np.random.permutation(T)[:J]
    idx3 = np.random.permutation(T)[:J]
    fk = mx_kscale(K)
    wp = pack_weight(n((K, N)) * 1 / np.sqrt(K) * fk[:, None], "e2m1")
    return {
        "xt": (n((K, T)) / fk[:, None]).astype(np.float32),
        "w_words": wp[0],
        "w_scales": wp[1],
        "mg": (np.random.uniform(0.2, 1.0, (N, 1))).astype(np.float32),
        "offs": striped(idx),
        "offs2": striped(idx2),
        "offs3": striped(idx3),
    }


def reference(xt, w_words, w_scales, mg, offs, offs2, offs3):
    idx = unstriped(offs)
    idx2 = unstriped(offs2)
    idx3 = unstriped(offs3)
    wu = unpack_weight(w_words, w_scales, "e2m1")
    xtidxq = mxq(f64(xt)[:, idx], 0, "e4m3")
    a = wu.T @ xtidxq
    xtidx2q = mxq(f64(xt)[:, idx2], 0, "e4m3")
    b = wu.T @ xtidx2q
    xtidx3q = mxq(f64(xt)[:, idx3], 0, "e4m3")
    e = wu.T @ xtidx3q
    y = softplus(0.3 * np.square(a - b) - 0.3 * np.square(a - e) + f64(mg))
    words, scales = planes(y)
    return y, words, scales

@@ -1,0 +1,199 @@
+import math
+from contextlib import ExitStack
+
+import concourse.mybir as mybir
+
+K, T, J, N = 512, 2048, 512, 512
+FLOPS = 3 * 2 * K * N * J
+
+F32 = mybir.dt.float32
+BF16 = mybir.dt.bfloat16
+I32 = mybir.dt.int32
+U32 = mybir.dt.uint32
+U16 = mybir.dt.uint16
+U8 = mybir.dt.uint8
+FP8X4 = mybir.dt.float8_e4m3fn_x4
+FP4X4 = mybir.dt.float4_e2m1fn_x4
+ALU = mybir.AluOpType
+ACT = mybir.ActivationFunctionType
+
+P = 128
+PACK = 4
+HALF = J // 2
+NARROW = 128
+EXP_CAP = 2.0 ** 60
+LOADS = ((512, 512, 512, 512), (512, 512, 512, 256, 256))
+SCALAR_CASTS = 3
+
+
+def tile_list_anchor_near_and_far_pl_kernel(tc, xt, w_words, w_scales, mg, offs, offs2, offs3, out_0, out_1, out_2):
+    nc = tc.nc
+    with ExitStack() as ctx:
+        keep = ctx.enter_context(tc.tile_pool(name="keep", bufs=1))
+        psum = ctx.enter_context(tc.psum_pool(name="psum", bufs=7))
+        psum_a = ctx.enter_context(tc.psum_pool(name="psum_a", bufs=1))
+
+        xt_rows = xt.rearrange("(p r) c -> p r c", r=PACK)
+        pairs = [keep.tile([P, T], F32, name="pairs%d" % u) for u in range(2)]
+
+        def load_x(u, i):
+            c0, width = sum(LOADS[u][:i]), LOADS[u][i]
+            raw = keep.tile([P, 2, width], F32, name="raw%d_%d" % (u, i))
+            nc.sync.dma_start(raw[:], xt_rows[:, 2 * u : 2 * u + 2, c0 : c0 + width])
+            return raw
+
+        def cast_x(u, i, raw):
+            c0, width = sum(LOADS[u][:i]), LOADS[u][i]
+            dst = pairs[u][:, c0 : c0 + width].bitcast(BF16).rearrange("p (c e) -> p c e", e=2)
+            src = raw[:].rearrange("p e c -> p c e")
+            if u == 1 and i < SCALAR_CASTS:
+                nc.scalar.copy(dst, src)
+            else:
+                nc.vector.tensor_copy(dst, src)
+
+        ws_raw = keep.tile([P, N], U8, name="ws_raw")
+        nc.gpsimd.memset(ws_raw[:].bitcast(I32), 0)
+        for q in range(4):
+            nc.scalar.dma_start(ws_raw[32 * q : 32 * q + 4, :].bitcast(I32), w_scales[0, 4 * q : 4 * q + 4, :].bitcast(I32))
+
+        w_raw = keep.tile([P, 2 * N], U8, name="w_raw")
+        nc.sync.dma_start(w_raw[:].bitcast(I32), w_words[0].bitcast(I32))
+        raws = [[load_x(0, i) for i in range(len(LOADS[0]))]]
+        lists = []
+        for name, src in (("anchor", offs), ("near", offs2), ("far", offs3)):
+            lst = keep.tile([P, J // 16], U16, name="list_" + name)
+            nc.sync.dma_start(lst[:], src)
+            lists.append(lst)
+        raws.append([load_x(1, i) for i in range(len(LOADS[1]))])
+        margin = keep.tile([P, PACK], F32, name="margin")
+        nc.sync.dma_start(margin[:], mg.rearrange("(p r) o -> p (r o)", r=PACK))
+
+        w_codes = keep.tile([P, PACK, P, 2], U8, name="w_codes", align_bytes=64)
+        w_plane = keep.tile([P, PACK, P], U8, name="w_plane", align_bytes=64)
+
+        nc.vector.tensor_copy(w_codes[:], w_raw[:].rearrange("p (m r b) -> p r m b", r=PACK, b=2))
+        cast_x(0, 0, raws[0][0])
+        nc.vector.tensor_copy(w_plane[:], ws_raw[:].rearrange("p (m r) -> p r m", r=PACK))
+        for i, raw in enumerate(raws[0][1:]):
+            cast_x(0, i + 1, raw)
+
+        first = [keep.tile([P, 2, HALF], F32, name="first%d" % l) for l in range(3)]
+        anchor_room = keep.tile([P, 3, HALF], F32, name="anchor_room", align_bytes=64)
+        others_room = keep.tile([P, 2, 2, HALF], F32, name="others_room", align_bytes=64)
+        picked = [[t[:] for t in first], [anchor_room[:, 0:2, :], others_room[:, :, 0, :], others_room[:, :, 1, :]]]
+
+        def gather(u, h, l):
+            cols = slice(h * HALF // 16, (h + 1) * HALF // 16)
+            nc.vector.tensor_copy(picked[h][l][:, u, :], pairs[u][:].indirect(lists[l][:, cols]))
+
+        for h in range(2):
+            for l in range(3):
+                gather(0, h, l)
+        for i, raw in enumerate(raws[1]):
+            cast_x(1, i, raw)
+
+        woven = [[keep.tile([P, HALF * PACK], BF16, name="woven%d_%d" % (h, l), align_bytes=64)[:] for l in range(3)] for h in range(2)]
+        woven[0][0] = anchor_room[:, 1:3, :].rearrange("p a j -> p (a j)").bitcast(BF16)
+        woven[0][2] = others_room[:, 1].rearrange("p a j -> p (a j)").bitcast(BF16)
+        x_codes = [[keep.tile([P, HALF], U32, name="x_codes%d_%d" % (h, l), align_bytes=64) for l in range(3)] for h in range(2)]
+        x_plane = [[keep.tile([P, HALF], U8, name="x_plane%d_%d" % (h, l), align_bytes=64) for l in range(3)] for h in range(2)]
+
+        def weave(h, l):
+            if l == 0:
+                src = picked[h][l].rearrange("p u j -> p (u j)").bitcast(BF16).rearrange("p (u j e) -> p j u e", u=2, e=2)
+                dst = woven[h][l].rearrange("p (j u e) -> p j u e", u=2, e=2)
+                nc.scalar.activation(dst, src, ACT.Copy, scale=-1.0)
+            else:
+                src = picked[h][l].rearrange("p u j -> p j u")
+                dst = woven[h][l].bitcast(F32).rearrange("p (j u) -> p j u", u=2)
+                nc.scalar.copy(dst, src)
+
+        def quantize(h, l):
+            nc.vector.quantize_mx(out=x_codes[h][l][:].bitcast(FP8X4), scales=x_plane[h][l][:], in_=woven[h][l])
+
+        def product(dst, r, h, l, cols, start, stop):
+            nc.tensor.matmul_mx(
+                out=dst,
+                lhsT=w_codes[:, r].rearrange("p m b -> p (m b)").bitcast(FP4X4),
+                lhsT_scale=w_plane[:, r, :],
+                rhs=x_codes[h][l][:, cols].bitcast(FP8X4),
+                rhs_scale=x_plane[h][l][:, cols],
+                start=start,
+                stop=stop,
+            )
+
+        z = keep.tile([P, PACK, J], F32, name="z")
+        grown = keep.tile([P, PACK, J], F32, name="grown")
+        root = math.sqrt(0.3)
+
+        def gaps(h):
+            whole = slice(0, HALF)
+            js = slice(h * HALF, (h + 1) * HALF)
+            anchor_ps = psum_a.tile([P, HALF], F32, name="anchor_ps")
+            product(anchor_ps[:], 0, h, 0, whole, True, True)
+            banks = [psum.tile([P, 2, HALF], F32, name="bank") for r in range(PACK)]
+            for side in range(2):
+                product(banks[0][:, side, :], 0, h, 1 + side, whole, True, True)
+            for r in range(1, PACK):
+                for side in range(2):
+                    for c0 in range(0, HALF, NARROW):
+                        cols = slice(c0, c0 + NARROW)
+                        product(banks[r][:, side, cols], r, h, 0, cols, True, False)
+                        product(banks[r][:, side, cols], r, h, 1 + side, cols, False, True)
+            anchor_sb = keep.tile([P, HALF], F32, name="anchor_sb%d" % h)
+            nc.vector.tensor_copy(anchor_sb[:], anchor_ps[:])
+            gap0 = keep.tile([P, 2, HALF], F32, name="gap0_%d" % h)
+            for side in range(2):
+                nc.vector.tensor_tensor(gap0[:, side, :], banks[0][:, side, :], anchor_sb[:], ALU.add)
+            for r in (1, 0, 2, 3):
+                squares = keep.tile([P, 2, HALF], F32, name="squares%d_%d" % (h, r))
+                if r == 0 and h == 1:
+                    nc.vector.scalar_tensor_tensor(squares[:], gap0[:], 0.3, gap0[:], ALU.mult, ALU.mult)
+                else:
+                    nc.scalar.activation(squares[:], gap0[:] if r == 0 else banks[r][:], ACT.Square, scale=root)
+                nc.vector.scalar_tensor_tensor(z[:, r, js], squares[:, 0, :], margin[:, r : r + 1], squares[:, 1, :], ALU.add, ALU.subtract)
+            for rs in (slice(0, 2), slice(2, 4)):
+                nc.scalar.activation(grown[:, rs, js], z[:, rs, js], ACT.Exp)
+
+        for l in range(3):
+            gather(1, 0, l)
+            weave(0, l)
+        quantize(0, 0)
+        gather(1, 1, 0)
+        quantize(0, 1)
+        quantize(0, 2)
+        gather(1, 1, 1)
+        gather(1, 1, 2)
+        for l in range(3):
+            weave(1, l)
+        for l in range(3):
+            quantize(1, l)
+        gaps(0)
+        gaps(1)
+
+        capped = keep.tile([P, PACK, J], F32, name="capped")
+        nc.vector.tensor_scalar(capped[:], grown[:], EXP_CAP, 1.0, ALU.min, ALU.add)
+
+        y = keep.tile([P, PACK, J], F32, name="y")
+        logs = keep.tile([P, PACK, J], F32, name="logs")
+        y_rows = out_0.rearrange("(p r) j -> p r j", r=PACK)
+        for h in range(2):
+            js = slice(h * HALF, (h + 1) * HALF)
+            for rs in (slice(0, 2), slice(2, 4)):
+                nc.scalar.activation(logs[:, rs, js], capped[:, rs, js], ACT.Ln)
+                nc.vector.tensor_tensor(y[:, rs, js], logs[:, rs, js], z[:, rs, js], ALU.max)
+                nc.sync.dma_start(y_rows[:, rs, js], y[:, rs, js])
+
+        y_codes = keep.tile([P, J], U32, name="y_codes", align_bytes=64)
+        y_plane = keep.tile([P, J], U8, name="y_plane", align_bytes=64)
+        words = out_1[0].rearrange("p c r -> p (c r)").bitcast(I32)
+        y_woven = [keep.tile([P, HALF, PACK], BF16, name="y_woven%d" % h, align_bytes=64) for h in range(2)]
+        nc.scalar.copy(y_woven[0][:], y[:, :, 0:HALF].rearrange("p r j -> p j r"))
+        nc.vector.tensor_copy(y_woven[1][:], y[:, :, HALF:J].rearrange("p r j -> p j r"))
+        for h in (0, 1):
+            js = slice(h * HALF, (h + 1) * HALF)
+            nc.vector.quantize_mx(out=y_codes[:, js].bitcast(FP8X4), scales=y_plane[:, js], in_=y_woven[h][:].rearrange("p j r -> p (j r)"))
+            nc.sync.dma_start(words[:, js], y_codes[:, js].bitcast(I32))
+        for q in range(4):
+            queue = nc.sync if q % 2 == 0 else nc.scalar
+            queue.dma_start(out_2[0, 4 * q : 4 * q + 4, :].bitcast(I32), y_plane[32 * q : 32 * q + 4, :].bitcast(I32))

@@ -22,8 +22,8 @@ PACK = 4
 HALF = J // 2
 NARROW = 128
 EXP_CAP = 2.0 ** 60
-LOADS = ((512, 512, 512, 512), (512, 512, 512, 256, 256))
-SCALAR_CASTS = 3
+LOADS = ((1024, 768, 256), (512, 512, 512, 256, 256))
+SCALAR_COLUMNS = ((352, 256, 80), (512, 512, 512, 0, 80))
 
 
 def tile_list_anchor_near_and_far_pl_kernel(tc, xt, w_words, w_scales, mg, offs, offs2, offs3, out_0, out_1, out_2):
@@ -46,15 +46,16 @@ def tile_list_anchor_near_and_far_pl_kernel(tc, xt, w_words, w_scales, mg, offs,
             c0, width = sum(LOADS[u][:i]), LOADS[u][i]
             dst = pairs[u][:, c0 : c0 + width].bitcast(BF16).rearrange("p (c e) -> p c e", e=2)
             src = raw[:].rearrange("p e c -> p c e")
-            if u == 1 and i < SCALAR_CASTS:
-                nc.scalar.copy(dst, src)
-            else:
-                nc.vector.tensor_copy(dst, src)
+            share = SCALAR_COLUMNS[u][i]
+            if share > 0:
+                nc.scalar.copy(dst[:, :share], src[:, :share])
+            if share < width:
+                nc.vector.tensor_copy(dst[:, share:], src[:, share:])
 
         ws_raw = keep.tile([P, N], U8, name="ws_raw")
         nc.gpsimd.memset(ws_raw[:].bitcast(I32), 0)
         for q in range(4):
-            nc.scalar.dma_start(ws_raw[32 * q : 32 * q + 4, :].bitcast(I32), w_scales[0, 4 * q : 4 * q + 4, :].bitcast(I32))
+            nc.gpsimd.dma_start(ws_raw[32 * q : 32 * q + 4, :].bitcast(I32), w_scales[0, 4 * q : 4 * q + 4, :].bitcast(I32))
 
         w_raw = keep.tile([P, 2 * N], U8, name="w_raw")
         nc.sync.dma_start(w_raw[:].bitcast(I32), w_words[0].bitcast(I32))
@@ -72,15 +73,14 @@ def tile_list_anchor_near_and_far_pl_kernel(tc, xt, w_words, w_scales, mg, offs,
         w_plane = keep.tile([P, PACK, P], U8, name="w_plane", align_bytes=64)
 
         nc.vector.tensor_copy(w_codes[:], w_raw[:].rearrange("p (m r b) -> p r m b", r=PACK, b=2))
-        cast_x(0, 0, raws[0][0])
-        nc.vector.tensor_copy(w_plane[:], ws_raw[:].rearrange("p (m r) -> p r m", r=PACK))
-        for i, raw in enumerate(raws[0][1:]):
-            cast_x(0, i + 1, raw)
+        nc.gpsimd.tensor_copy(w_plane[:], ws_raw[:].rearrange("p (m r) -> p r m", r=PACK))
+        for i, raw in enumerate(raws[0]):
+            cast_x(0, i, raw)
 
         first = [keep.tile([P, 2, HALF], F32, name="first%d" % l) for l in range(3)]
-        anchor_room = keep.tile([P, 3, HALF], F32, name="anchor_room", align_bytes=64)
+        anchor_room = keep.tile([P, 2, HALF], F32, name="anchor_room")
         others_room = keep.tile([P, 2, 2, HALF], F32, name="others_room", align_bytes=64)
-        picked = [[t[:] for t in first], [anchor_room[:, 0:2, :], others_room[:, :, 0, :], others_room[:, :, 1, :]]]
+        picked = [[t[:] for t in first], [anchor_room[:], others_room[:, :, 0, :], others_room[:, :, 1, :]]]
 
         def gather(u, h, l):
             cols = slice(h * HALF // 16, (h + 1) * HALF // 16)
@@ -93,7 +93,6 @@ def tile_list_anchor_near_and_far_pl_kernel(tc, xt, w_words, w_scales, mg, offs,
             cast_x(1, i, raw)
 
         woven = [[keep.tile([P, HALF * PACK], BF16, name="woven%d_%d" % (h, l), align_bytes=64)[:] for l in range(3)] for h in range(2)]
-        woven[0][0] = anchor_room[:, 1:3, :].rearrange("p a j -> p (a j)").bitcast(BF16)
         woven[0][2] = others_room[:, 1].rearrange("p a j -> p (a j)").bitcast(BF16)
         x_codes = [[keep.tile([P, HALF], U32, name="x_codes%d_%d" % (h, l), align_bytes=64) for l in range(3)] for h in range(2)]
         x_plane = [[keep.tile([P, HALF], U8, name="x_plane%d_%d" % (h, l), align_bytes=64) for l in range(3)] for h in range(2)]
@@ -106,7 +105,10 @@ def tile_list_anchor_near_and_far_pl_kernel(tc, xt, w_words, w_scales, mg, offs,
             else:
                 src = picked[h][l].rearrange("p u j -> p j u")
                 dst = woven[h][l].bitcast(F32).rearrange("p (j u) -> p j u", u=2)
-                nc.scalar.copy(dst, src)
+                if (h, l) == (1, 1):
+                    nc.vector.tensor_copy(dst, src)
+                else:
+                    nc.scalar.copy(dst, src)
 
         def quantize(h, l):
             nc.vector.quantize_mx(out=x_codes[h][l][:].bitcast(FP8X4), scales=x_plane[h][l][:], in_=woven[h][l])
@@ -132,42 +134,35 @@ def tile_list_anchor_near_and_far_pl_kernel(tc, xt, w_words, w_scales, mg, offs,
             anchor_ps = psum_a.tile([P, HALF], F32, name="anchor_ps")
             product(anchor_ps[:], 0, h, 0, whole, True, True)
             banks = [psum.tile([P, 2, HALF], F32, name="bank") for r in range(PACK)]
-            for side in range(2):
-                product(banks[0][:, side, :], 0, h, 1 + side, whole, True, True)
-            for r in range(1, PACK):
+            for r in (1, 0, 2, 3):
                 for side in range(2):
+                    if r == 0:
+                        product(banks[0][:, side, :], 0, h, 1 + side, whole, True, True)
+                        continue
                     for c0 in range(0, HALF, NARROW):
                         cols = slice(c0, c0 + NARROW)
                         product(banks[r][:, side, cols], r, h, 0, cols, True, False)
                         product(banks[r][:, side, cols], r, h, 1 + side, cols, False, True)
             anchor_sb = keep.tile([P, HALF], F32, name="anchor_sb%d" % h)
-            nc.vector.tensor_copy(anchor_sb[:], anchor_ps[:])
+            nc.scalar.copy(anchor_sb[:], anchor_ps[:])
             gap0 = keep.tile([P, 2, HALF], F32, name="gap0_%d" % h)
-            for side in range(2):
-                nc.vector.tensor_tensor(gap0[:, side, :], banks[0][:, side, :], anchor_sb[:], ALU.add)
-            for r in (1, 0, 2, 3):
+            nc.vector.tensor_tensor(gap0[:], banks[0][:], anchor_sb[:].unsqueeze(1).to_broadcast([P, 2, HALF]), ALU.add)
+            for r in (1, 2, 0, 3):
                 squares = keep.tile([P, 2, HALF], F32, name="squares%d_%d" % (h, r))
-                if r == 0 and h == 1:
+                if r == 0:
                     nc.vector.scalar_tensor_tensor(squares[:], gap0[:], 0.3, gap0[:], ALU.mult, ALU.mult)
                 else:
-                    nc.scalar.activation(squares[:], gap0[:] if r == 0 else banks[r][:], ACT.Square, scale=root)
+                    nc.scalar.activation(squares[:], banks[r][:], ACT.Square, scale=root)
                 nc.vector.scalar_tensor_tensor(z[:, r, js], squares[:, 0, :], margin[:, r : r + 1], squares[:, 1, :], ALU.add, ALU.subtract)
-            for rs in (slice(0, 2), slice(2, 4)):
+            for rs in (slice(0, 4),) if h == 0 else (slice(1, 3), slice(0, 1), slice(3, 4)):
                 nc.scalar.activation(grown[:, rs, js], z[:, rs, js], ACT.Exp)
 
-        for l in range(3):
-            gather(1, 0, l)
-            weave(0, l)
-        quantize(0, 0)
-        gather(1, 1, 0)
-        quantize(0, 1)
-        quantize(0, 2)
-        gather(1, 1, 1)
-        gather(1, 1, 2)
-        for l in range(3):
-            weave(1, l)
-        for l in range(3):
-            quantize(1, l)
+        for h in range(2):
+            for l in range(3):
+                gather(1, h, l)
+                weave(h, l)
+            for l in range(3):
+                quantize(h, l)
         gaps(0)
         gaps(1)
 
@@ -179,17 +174,19 @@ def tile_list_anchor_near_and_far_pl_kernel(tc, xt, w_words, w_scales, mg, offs,
         y_rows = out_0.rearrange("(p r) j -> p r j", r=PACK)
         for h in range(2):
             js = slice(h * HALF, (h + 1) * HALF)
-            for rs in (slice(0, 2), slice(2, 4)):
-                nc.scalar.activation(logs[:, rs, js], capped[:, rs, js], ACT.Ln)
-                nc.vector.tensor_tensor(y[:, rs, js], logs[:, rs, js], z[:, rs, js], ALU.max)
+            for r0 in (0, 2):
+                rs = slice(r0, r0 + 2)
+                for part in (slice(0, 1), slice(1, 2)) if (h, r0) == (0, 0) else (rs,):
+                    nc.scalar.activation(logs[:, part, js], capped[:, part, js], ACT.Ln)
+                    nc.vector.tensor_tensor(y[:, part, js], logs[:, part, js], z[:, part, js], ALU.max)
                 nc.sync.dma_start(y_rows[:, rs, js], y[:, rs, js])
 
         y_codes = keep.tile([P, J], U32, name="y_codes", align_bytes=64)
         y_plane = keep.tile([P, J], U8, name="y_plane", align_bytes=64)
         words = out_1[0].rearrange("p c r -> p (c r)").bitcast(I32)
         y_woven = [keep.tile([P, HALF, PACK], BF16, name="y_woven%d" % h, align_bytes=64) for h in range(2)]
-        nc.scalar.copy(y_woven[0][:], y[:, :, 0:HALF].rearrange("p r j -> p j r"))
-        nc.vector.tensor_copy(y_woven[1][:], y[:, :, HALF:J].rearrange("p r j -> p j r"))
+        nc.scalar.copy(y_woven[0][:].rearrange("p (c i) r -> p c r i", i=4), y[:, :, 0:HALF].rearrange("p r (c i) -> p c r i", i=4))
+        nc.vector.tensor_copy(y_woven[1][:].rearrange("p (c i) r -> p c r i", i=4), y[:, :, HALF:J].rearrange("p r (c i) -> p c r i", i=4))
         for h in (0, 1):
             js = slice(h * HALF, (h + 1) * HALF)
             nc.vector.quantize_mx(out=y_codes[:, js].bitcast(FP8X4), scales=y_plane[:, js], in_=y_woven[h][:].rearrange("p j r -> p (j r)"))

@@ -23,7 +23,7 @@ HALF = J // 2
 NARROW = 128
 EXP_CAP = 2.0 ** 60
 LOADS = ((1024, 768, 256), (512, 512, 512, 256, 256))
-SCALAR_COLUMNS = ((352, 256, 80), (512, 512, 512, 0, 80))
+SCALAR_COLUMNS = ((640, 256, 80), (512, 512, 512, 0, 80))
 
 
 def tile_list_anchor_near_and_far_pl_kernel(tc, xt, w_words, w_scales, mg, offs, offs2, offs3, out_0, out_1, out_2):
@@ -53,13 +53,13 @@ def tile_list_anchor_near_and_far_pl_kernel(tc, xt, w_words, w_scales, mg, offs,
                 nc.vector.tensor_copy(dst[:, share:], src[:, share:])
 
         ws_raw = keep.tile([P, N], U8, name="ws_raw")
-        nc.gpsimd.memset(ws_raw[:].bitcast(I32), 0)
+        nc.vector.memset(ws_raw[:].bitcast(I32), 0)
+        raws = [[load_x(0, 0)]]
         for q in range(4):
-            nc.gpsimd.dma_start(ws_raw[32 * q : 32 * q + 4, :].bitcast(I32), w_scales[0, 4 * q : 4 * q + 4, :].bitcast(I32))
-
+            nc.sync.dma_start(ws_raw[32 * q : 32 * q + 4, :].bitcast(I32), w_scales[0, 4 * q : 4 * q + 4, :].bitcast(I32))
         w_raw = keep.tile([P, 2 * N], U8, name="w_raw")
         nc.sync.dma_start(w_raw[:].bitcast(I32), w_words[0].bitcast(I32))
-        raws = [[load_x(0, i) for i in range(len(LOADS[0]))]]
+        raws[0].extend([load_x(0, i) for i in range(1, len(LOADS[0]))])
         lists = []
         for name, src in (("anchor", offs), ("near", offs2), ("far", offs3)):
             lst = keep.tile([P, J // 16], U16, name="list_" + name)
@@ -72,10 +72,11 @@ def tile_list_anchor_near_and_far_pl_kernel(tc, xt, w_words, w_scales, mg, offs,
         w_codes = keep.tile([P, PACK, P, 2], U8, name="w_codes", align_bytes=64)
         w_plane = keep.tile([P, PACK, P], U8, name="w_plane", align_bytes=64)
 
+        cast_x(0, 0, raws[0][0])
+        nc.vector.tensor_copy(w_plane[:], ws_raw[:].rearrange("p (m r) -> p r m", r=PACK))
         nc.vector.tensor_copy(w_codes[:], w_raw[:].rearrange("p (m r b) -> p r m b", r=PACK, b=2))
-        nc.gpsimd.tensor_copy(w_plane[:], ws_raw[:].rearrange("p (m r) -> p r m", r=PACK))
-        for i, raw in enumerate(raws[0]):
-            cast_x(0, i, raw)
+        for i in range(1, len(LOADS[0])):
+            cast_x(0, i, raws[0][i])
 
         first = [keep.tile([P, 2, HALF], F32, name="first%d" % l) for l in range(3)]
         anchor_room = keep.tile([P, 2, HALF], F32, name="anchor_room")
@@ -92,10 +93,12 @@ def tile_list_anchor_near_and_far_pl_kernel(tc, xt, w_words, w_scales, mg, offs,
         for i, raw in enumerate(raws[1]):
             cast_x(1, i, raw)
 
-        woven = [[keep.tile([P, HALF * PACK], BF16, name="woven%d_%d" % (h, l), align_bytes=64)[:] for l in range(3)] for h in range(2)]
-        woven[0][2] = others_room[:, 1].rearrange("p a j -> p (a j)").bitcast(BF16)
-        x_codes = [[keep.tile([P, HALF], U32, name="x_codes%d_%d" % (h, l), align_bytes=64) for l in range(3)] for h in range(2)]
-        x_plane = [[keep.tile([P, HALF], U8, name="x_plane%d_%d" % (h, l), align_bytes=64) for l in range(3)] for h in range(2)]
+        woven_anchor = [others_room[:, 1].rearrange("p a j -> p (a j)").bitcast(BF16),
+                        keep.tile([P, HALF * PACK], BF16, name="woven_anchor1", align_bytes=64)[:]]
+        woven_others = [keep.tile([P, 2, HALF * PACK], BF16, name="woven_others%d" % h, align_bytes=64) for h in range(2)]
+        woven = [[woven_anchor[h], woven_others[h][:, 0, :], woven_others[h][:, 1, :]] for h in range(2)]
+        x_codes = [[keep.tile([P, J], U32, name="x_codes%d_%d" % (h, g), align_bytes=64) for g in range(2)] for h in range(2)]
+        x_plane = [[keep.tile([P, J], U8, name="x_plane%d_%d" % (h, g), align_bytes=64) for g in range(2)] for h in range(2)]
 
         def weave(h, l):
             if l == 0:
@@ -105,13 +108,16 @@ def tile_list_anchor_near_and_far_pl_kernel(tc, xt, w_words, w_scales, mg, offs,
             else:
                 src = picked[h][l].rearrange("p u j -> p j u")
                 dst = woven[h][l].bitcast(F32).rearrange("p (j u) -> p j u", u=2)
-                if (h, l) == (1, 1):
+                if (h, l) == (1, 2):
                     nc.vector.tensor_copy(dst, src)
                 else:
                     nc.scalar.copy(dst, src)
 
-        def quantize(h, l):
-            nc.vector.quantize_mx(out=x_codes[h][l][:].bitcast(FP8X4), scales=x_plane[h][l][:], in_=woven[h][l])
+        def quantize(h):
+            for side in range(2):
+                cols = slice(side * HALF, (side + 1) * HALF)
+                nc.vector.quantize_mx(out=x_codes[h][0][:, cols].bitcast(FP8X4), scales=x_plane[h][0][:, cols], in_=woven[h][0])
+            nc.vector.quantize_mx(out=x_codes[h][1][:].bitcast(FP8X4), scales=x_plane[h][1][:], in_=woven_others[h][:].rearrange("p l c -> p (l c)"))
 
         def product(dst, r, h, l, cols, start, stop):
             nc.tensor.matmul_mx(
@@ -134,15 +140,11 @@ def tile_list_anchor_near_and_far_pl_kernel(tc, xt, w_words, w_scales, mg, offs,
             anchor_ps = psum_a.tile([P, HALF], F32, name="anchor_ps")
             product(anchor_ps[:], 0, h, 0, whole, True, True)
             banks = [psum.tile([P, 2, HALF], F32, name="bank") for r in range(PACK)]
-            for r in (1, 0, 2, 3):
-                for side in range(2):
-                    if r == 0:
-                        product(banks[0][:, side, :], 0, h, 1 + side, whole, True, True)
-                        continue
-                    for c0 in range(0, HALF, NARROW):
-                        cols = slice(c0, c0 + NARROW)
-                        product(banks[r][:, side, cols], r, h, 0, cols, True, False)
-                        product(banks[r][:, side, cols], r, h, 1 + side, cols, False, True)
+            for r in (1, 2, 3, 0):
+                bank = banks[r][:].rearrange("p s j -> p (s j)")
+                if r != 0:
+                    product(bank, r, h, 0, slice(0, J), True, False)
+                product(bank, r, h, 1, slice(0, J), r == 0, True)
             anchor_sb = keep.tile([P, HALF], F32, name="anchor_sb%d" % h)
             nc.scalar.copy(anchor_sb[:], anchor_ps[:])
             gap0 = keep.tile([P, 2, HALF], F32, name="gap0_%d" % h)
@@ -161,8 +163,7 @@ def tile_list_anchor_near_and_far_pl_kernel(tc, xt, w_words, w_scales, mg, offs,
             for l in range(3):
                 gather(1, h, l)
                 weave(h, l)
-            for l in range(3):
-                quantize(h, l)
+            quantize(h)
         gaps(0)
         gaps(1)
 

@@ -108,7 +108,7 @@ def tile_list_anchor_near_and_far_pl_kernel(tc, xt, w_words, w_scales, mg, offs,
             else:
                 src = picked[h][l].rearrange("p u j -> p j u")
                 dst = woven[h][l].bitcast(F32).rearrange("p (j u) -> p j u", u=2)
-                if (h, l) == (1, 2):
+                if h == 1:
                     nc.vector.tensor_copy(dst, src)
                 else:
                     nc.scalar.copy(dst, src)

import math
from contextlib import ExitStack

import concourse.mybir as mybir

K, T, J, N = 512, 2048, 512, 512
FLOPS = 3 * 2 * K * N * J

F32 = mybir.dt.float32
BF16 = mybir.dt.bfloat16
I32 = mybir.dt.int32
U32 = mybir.dt.uint32
U16 = mybir.dt.uint16
U8 = mybir.dt.uint8
FP8X4 = mybir.dt.float8_e4m3fn_x4
FP4X4 = mybir.dt.float4_e2m1fn_x4
ALU = mybir.AluOpType
ACT = mybir.ActivationFunctionType

P = 128
PACK = 4
HALF = J // 2
NARROW = 128
EXP_CAP = 2.0 ** 60
LOADS = ((1024, 768, 256), (512, 512, 512, 256, 256))
SCALAR_COLUMNS = ((640, 256, 80), (512, 512, 512, 0, 80))


def tile_list_anchor_near_and_far_pl_kernel(tc, xt, w_words, w_scales, mg, offs, offs2, offs3, out_0, out_1, out_2):
    nc = tc.nc
    with ExitStack() as ctx:
        keep = ctx.enter_context(tc.tile_pool(name="keep", bufs=1))
        psum = ctx.enter_context(tc.psum_pool(name="psum", bufs=7))
        psum_a = ctx.enter_context(tc.psum_pool(name="psum_a", bufs=1))

        xt_rows = xt.rearrange("(p r) c -> p r c", r=PACK)
        pairs = [keep.tile([P, T], F32, name="pairs%d" % u) for u in range(2)]

        def load_x(u, i):
            c0, width = sum(LOADS[u][:i]), LOADS[u][i]
            raw = keep.tile([P, 2, width], F32, name="raw%d_%d" % (u, i))
            nc.sync.dma_start(raw[:], xt_rows[:, 2 * u : 2 * u + 2, c0 : c0 + width])
            return raw

        def cast_x(u, i, raw):
            c0, width = sum(LOADS[u][:i]), LOADS[u][i]
            dst = pairs[u][:, c0 : c0 + width].bitcast(BF16).rearrange("p (c e) -> p c e", e=2)
            src = raw[:].rearrange("p e c -> p c e")
            share = SCALAR_COLUMNS[u][i]
            if share > 0:
                nc.scalar.copy(dst[:, :share], src[:, :share])
            if share < width:
                nc.vector.tensor_copy(dst[:, share:], src[:, share:])

        ws_raw = keep.tile([P, N], U8, name="ws_raw")
        nc.vector.memset(ws_raw[:].bitcast(I32), 0)
        raws = [[load_x(0, 0)]]
        for q in range(4):
            nc.sync.dma_start(ws_raw[32 * q : 32 * q + 4, :].bitcast(I32), w_scales[0, 4 * q : 4 * q + 4, :].bitcast(I32))
        w_raw = keep.tile([P, 2 * N], U8, name="w_raw")
        nc.sync.dma_start(w_raw[:].bitcast(I32), w_words[0].bitcast(I32))
        raws[0].extend([load_x(0, i) for i in range(1, len(LOADS[0]))])
        lists = []
        for name, src in (("anchor", offs), ("near", offs2), ("far", offs3)):
            lst = keep.tile([P, J // 16], U16, name="list_" + name)
            nc.sync.dma_start(lst[:], src)
            lists.append(lst)
        raws.append([load_x(1, i) for i in range(len(LOADS[1]))])
        margin = keep.tile([P, PACK], F32, name="margin")
        nc.sync.dma_start(margin[:], mg.rearrange("(p r) o -> p (r o)", r=PACK))

        w_codes = keep.tile([P, PACK, P, 2], U8, name="w_codes", align_bytes=64)
        w_plane = keep.tile([P, PACK, P], U8, name="w_plane", align_bytes=64)

        cast_x(0, 0, raws[0][0])
        nc.vector.tensor_copy(w_plane[:], ws_raw[:].rearrange("p (m r) -> p r m", r=PACK))
        nc.vector.tensor_copy(w_codes[:], w_raw[:].rearrange("p (m r b) -> p r m b", r=PACK, b=2))
        for i in range(1, len(LOADS[0])):
            cast_x(0, i, raws[0][i])

        first = [keep.tile([P, 2, HALF], F32, name="first%d" % l) for l in range(3)]
        anchor_room = keep.tile([P, 2, HALF], F32, name="anchor_room")
        others_room = keep.tile([P, 2, 2, HALF], F32, name="others_room", align_bytes=64)
        picked = [[t[:] for t in first], [anchor_room[:], others_room[:, :, 0, :], others_room[:, :, 1, :]]]

        def gather(u, h, l):
            cols = slice(h * HALF // 16, (h + 1) * HALF // 16)
            nc.vector.tensor_copy(picked[h][l][:, u, :], pairs[u][:].indirect(lists[l][:, cols]))

        for h in range(2):
            for l in range(3):
                gather(0, h, l)
        for i, raw in enumerate(raws[1]):
            cast_x(1, i, raw)

        woven_anchor = [others_room[:, 1].rearrange("p a j -> p (a j)").bitcast(BF16),
                        keep.tile([P, HALF * PACK], BF16, name="woven_anchor1", align_bytes=64)[:]]
        woven_others = [keep.tile([P, 2, HALF * PACK], BF16, name="woven_others%d" % h, align_bytes=64) for h in range(2)]
        woven = [[woven_anchor[h], woven_others[h][:, 0, :], woven_others[h][:, 1, :]] for h in range(2)]
        x_codes = [[keep.tile([P, J], U32, name="x_codes%d_%d" % (h, g), align_bytes=64) for g in range(2)] for h in range(2)]
        x_plane = [[keep.tile([P, J], U8, name="x_plane%d_%d" % (h, g), align_bytes=64) for g in range(2)] for h in range(2)]

        def weave(h, l):
            if l == 0:
                src = picked[h][l].rearrange("p u j -> p (u j)").bitcast(BF16).rearrange("p (u j e) -> p j u e", u=2, e=2)
                dst = woven[h][l].rearrange("p (j u e) -> p j u e", u=2, e=2)
                nc.scalar.activation(dst, src, ACT.Copy, scale=-1.0)
            else:
                src = picked[h][l].rearrange("p u j -> p j u")
                dst = woven[h][l].bitcast(F32).rearrange("p (j u) -> p j u", u=2)
                if h == 1:
                    nc.vector.tensor_copy(dst, src)
                else:
                    nc.scalar.copy(dst, src)

        def quantize(h):
            for side in range(2):
                cols = slice(side * HALF, (side + 1) * HALF)
                nc.vector.quantize_mx(out=x_codes[h][0][:, cols].bitcast(FP8X4), scales=x_plane[h][0][:, cols], in_=woven[h][0])
            nc.vector.quantize_mx(out=x_codes[h][1][:].bitcast(FP8X4), scales=x_plane[h][1][:], in_=woven_others[h][:].rearrange("p l c -> p (l c)"))

        def product(dst, r, h, l, cols, start, stop):
            nc.tensor.matmul_mx(
                out=dst,
                lhsT=w_codes[:, r].rearrange("p m b -> p (m b)").bitcast(FP4X4),
                lhsT_scale=w_plane[:, r, :],
                rhs=x_codes[h][l][:, cols].bitcast(FP8X4),
                rhs_scale=x_plane[h][l][:, cols],
                start=start,
                stop=stop,
            )

        z = keep.tile([P, PACK, J], F32, name="z")
        grown = keep.tile([P, PACK, J], F32, name="grown")
        root = math.sqrt(0.3)

        def gaps(h):
            whole = slice(0, HALF)
            js = slice(h * HALF, (h + 1) * HALF)
            anchor_ps = psum_a.tile([P, HALF], F32, name="anchor_ps")
            product(anchor_ps[:], 0, h, 0, whole, True, True)
            banks = [psum.tile([P, 2, HALF], F32, name="bank") for r in range(PACK)]
            for r in (1, 2, 3, 0):
                bank = banks[r][:].rearrange("p s j -> p (s j)")
                if r != 0:
                    product(bank, r, h, 0, slice(0, J), True, False)
                product(bank, r, h, 1, slice(0, J), r == 0, True)
            anchor_sb = keep.tile([P, HALF], F32, name="anchor_sb%d" % h)
            nc.scalar.copy(anchor_sb[:], anchor_ps[:])
            gap0 = keep.tile([P, 2, HALF], F32, name="gap0_%d" % h)
            nc.vector.tensor_tensor(gap0[:], banks[0][:], anchor_sb[:].unsqueeze(1).to_broadcast([P, 2, HALF]), ALU.add)
            for r in (1, 2, 0, 3):
                squares = keep.tile([P, 2, HALF], F32, name="squares%d_%d" % (h, r))
                if r == 0:
                    nc.vector.scalar_tensor_tensor(squares[:], gap0[:], 0.3, gap0[:], ALU.mult, ALU.mult)
                else:
                    nc.scalar.activation(squares[:], banks[r][:], ACT.Square, scale=root)
                nc.vector.scalar_tensor_tensor(z[:, r, js], squares[:, 0, :], margin[:, r : r + 1], squares[:, 1, :], ALU.add, ALU.subtract)
            for rs in (slice(0, 4),) if h == 0 else (slice(1, 3), slice(0, 1), slice(3, 4)):
                nc.scalar.activation(grown[:, rs, js], z[:, rs, js], ACT.Exp)

        for h in range(2):
            for l in range(3):
                gather(1, h, l)
                weave(h, l)
            quantize(h)
        gaps(0)
        gaps(1)

        capped = keep.tile([P, PACK, J], F32, name="capped")
        nc.vector.tensor_scalar(capped[:], grown[:], EXP_CAP, 1.0, ALU.min, ALU.add)

        y = keep.tile([P, PACK, J], F32, name="y")
        logs = keep.tile([P, PACK, J], F32, name="logs")
        y_rows = out_0.rearrange("(p r) j -> p r j", r=PACK)
        for h in range(2):
            js = slice(h * HALF, (h + 1) * HALF)
            for r0 in (0, 2):
                rs = slice(r0, r0 + 2)
                for part in (slice(0, 1), slice(1, 2)) if (h, r0) == (0, 0) else (rs,):
                    nc.scalar.activation(logs[:, part, js], capped[:, part, js], ACT.Ln)
                    nc.vector.tensor_tensor(y[:, part, js], logs[:, part, js], z[:, part, js], ALU.max)
                nc.sync.dma_start(y_rows[:, rs, js], y[:, rs, js])

        y_codes = keep.tile([P, J], U32, name="y_codes", align_bytes=64)
        y_plane = keep.tile([P, J], U8, name="y_plane", align_bytes=64)
        words = out_1[0].rearrange("p c r -> p (c r)").bitcast(I32)
        y_woven = [keep.tile([P, HALF, PACK], BF16, name="y_woven%d" % h, align_bytes=64) for h in range(2)]
        nc.scalar.copy(y_woven[0][:].rearrange("p (c i) r -> p c r i", i=4), y[:, :, 0:HALF].rearrange("p r (c i) -> p c r i", i=4))
        nc.vector.tensor_copy(y_woven[1][:].rearrange("p (c i) r -> p c r i", i=4), y[:, :, HALF:J].rearrange("p r (c i) -> p c r i", i=4))
        for h in (0, 1):
            js = slice(h * HALF, (h + 1) * HALF)
            nc.vector.quantize_mx(out=y_codes[:, js].bitcast(FP8X4), scales=y_plane[:, js], in_=y_woven[h][:].rearrange("p j r -> p (j r)"))
            nc.sync.dma_start(words[:, js], y_codes[:, js].bitcast(I32))
        for q in range(4):
            queue = nc.sync if q % 2 == 0 else nc.scalar
            queue.dma_start(out_2[0, 4 * q : 4 * q + 4, :].bitcast(I32), y_plane[32 * q : 32 * q + 4, :].bitcast(I32))
